import numpy as np, ml_dtypes
CORES = [10,34,74,98]
N = 4
T, CAP, KR = 512, 192, 1024
def entries(a): return a.T.reshape(-1)
def pack(v, P): return np.ascontiguousarray(np.asarray(v, np.int32).reshape(-1, P).T)
def lists(rng, how):
    D = np.stack([rng.permutation(np.repeat(np.arange(N), CAP))[:T] for r in range(N)])
    if how == "full": D = np.stack([(lambda q: rng.permutation(np.concatenate([np.repeat(q[:T // CAP], CAP), np.repeat(q[T // CAP:T // CAP + 1], T % CAP)])))(rng.permutation(N)) for r in range(N)])
    if how == "sorted": D = np.sort(D, axis=1)
    if how == "none": z = int(rng.integers(N)); D = np.stack([rng.permutation(np.repeat(np.delete(np.arange(N), z), CAP))[:T] for r in range(N)]) if CAP * (N - 1) >= T else D
    K_ = KR * D + (np.where(rng.random((N, T)) < 0.5, 0, KR - 1) if how == "edge" else rng.integers(0, KR, (N, T)))
    return {"key": np.stack([pack(K_[r], 16) for r in range(N)])}
def setup_inputs(rng):
    return dict({"x": rng.standard_normal((N, 128, T), dtype=np.float32).astype(ml_dtypes.bfloat16)}, **lists(rng, "uniform"))
def setup_inputs_edge(rng):
    d = setup_inputs(rng); d.update(lists(rng, "edge"))
    for k in ("x",): d[k] = (d[k].astype(np.float32) * 1048576.0).astype(d[k].dtype)
    return d
def setup_inputs_full(rng):
    d = setup_inputs(rng); d.update(lists(rng, "full"))
    for k in ("x",): d[k] = (d[k].astype(np.float32) * (1 / 1024.0)).astype(d[k].dtype)
    return d
def setup_inputs_none(rng):
    d = setup_inputs(rng); d.update(lists(rng, "none"))
    return d
def setup_inputs_sorted(rng):
    d = setup_inputs(rng); d.update(lists(rng, "sorted"))
    return d
def check_inputs(x):
    bad = []
    if x["key"].min() < 0 or x["key"].max() >= N * KR: bad.append("key out of range")
    if max(int(np.bincount(entries(a) // KR, minlength=N).max()) for a in x["key"]) > CAP: bad.append("more than CAP columns of a rank go to one rank")
    return bad
def reference(x, key):
    y = np.zeros((N, 128, N * CAP), x.dtype)
    for r in range(N):
        D = entries(key[r]) // KR
        for d in range(N):
            got = x[r][:, D == d]; y[d][:, CAP * r:CAP * r + got.shape[1]] = got
    return {"y": y}

@@ -1,0 +1,144 @@
+from concourse.mybir import AluOpType
+
+N = 4
+CAP = 192
+COLS = 512
+WIN = N * CAP
+
+SCRATCH = {
+    "xs": ("sbuf", [128, COLS], "bfloat16"),
+    "win": ("sbuf", [128, WIN], "bfloat16"),
+    "land": ("sbuf", [128, WIN], "bfloat16"),
+    "kk": ("sbuf", [128, 32], "int32"),
+    "dd": ("sbuf", [128, 32], "int32"),
+    "mm": ("sbuf", [128, 33], "bfloat16"),
+    "z0": ("sbuf", [128, 32], "float32"),
+    "ta": ("sbuf", [128, 64], "int32"),
+    "ea": ("sbuf", [128, 64], "int32"),
+    "a1": ("sbuf", [128, 64], "bfloat16"),
+    "a2": ("sbuf", [128, 64], "bfloat16"),
+    "tr": ("sbuf", [128, 128], "int32"),
+    "er": ("sbuf", [128, 128], "int32"),
+    "rep": ("sbuf", [128, 128], "bfloat16"),
+    "rep192": ("sbuf", [128, 128], "bfloat16"),
+    "di": ("sbuf", [128, 1], "int32"),
+    "dcol": ("sbuf", [128, 1], "float32"),
+    "d192": ("sbuf", [128, 1], "float32"),
+    "sc": ("sbuf", [128, 32], "float32"),
+    "pr": ("sbuf", [128, 32], "bfloat16"),
+    "off": ("sbuf", [128, 32], "uint16"),
+    "ps1": ("psum", [128, 512], "float32"),
+    "ps2": ("psum", [128, 512], "float32"),
+}
+SEMAPHORES = ["s%d" % i for i in range(32)] + ["kld", "xld", "st", "sent"] + ["arr%d" % i for i in range(N)]
+
+
+def rank_program(g, core, T, topo):
+    rank = T.rank_of(core)
+    if rank is None:
+        return
+    V, PE, SY, SC = g.vector, g.tensor, g.sync, g.scalar
+    A = AluOpType
+    used = [0]
+
+    def new():
+        used[0] += 1
+        return T.sem["s%d" % (used[0] - 1)]
+
+    K = 4 * 16
+
+    for d in range(N):
+        q = SY if d < 2 else SC
+        q.dma_start(T.kk[d:K:4, :], T.key[:, :]).then_inc(T.sem.kld, 16)
+    SY.dma_start(T.xs[:, :], T.x[:, :]).then_inc(T.sem.xld, 16)
+
+    s_ta, s_tr, s_wg = new(), new(), new()
+    g.iota(T.ta[0:K, :], [[-1, 64]], 64, 1).then_inc(s_ta, 1)
+    g.iota(T.tr[0:K, :], [[0, 8], [4, 16]], 67, -1).then_inc(s_tr, 1)
+    half = WIN // 2
+    g.iota(T.win[:, half:WIN], [[0, WIN - half]], 0, 0, allow_small_or_imprecise_dtypes=True).then_inc(s_wg, 1)
+
+    s_m0, s_z0, s_wv = new(), new(), new()
+    V.memset(T.mm[0:K, 0:1], 0.0).then_inc(s_m0, 1)
+    V.memset(T.z0[0:K, :], 0.0).then_inc(s_z0, 1)
+    V.memset(T.win[:, 0:half], 0.0).then_inc(s_wv, 1)
+    s_di, s_ea, s_dcol, s_d192, s_a1, s_a2, s_er, s_r192, s_rep = [new() for _ in range(9)]
+    V.wait_ge(s_ta, 1)
+    V.tensor_scalar(T.di[0:K, :], T.ta[0:K, 0:1], 3, None, A.bitwise_and).then_inc(s_di, 1)
+    V.tensor_scalar(T.ea[0:K, :], T.ta[0:K, :], 67, None, A.bitwise_and).then_inc(s_ea, 1)
+    V.wait_ge(s_di, 1)
+    V.tensor_copy(T.dcol[0:K, :], T.di[0:K, :]).then_inc(s_dcol, 1)
+    V.tensor_scalar(T.d192[0:K, :], T.di[0:K, :], float(CAP), None, A.mult).then_inc(s_d192, 1)
+    V.wait_ge(s_ea, 1)
+    V.tensor_scalar(T.a1[0:K, :], T.ea[0:K, :], 0.0, None, A.is_equal).then_inc(s_a1, 1)
+    V.tensor_scalar(T.a2[0:K, :], T.ea[0:K, :], 64.0, None, A.is_equal).then_inc(s_a2, 1)
+    V.wait_ge(s_tr, 1)
+    V.tensor_scalar(T.er[0:K, :], T.tr[0:K, :], 124, None, A.bitwise_and).then_inc(s_er, 1)
+    V.wait_ge(s_er, 1)
+    V.wait_ge(s_d192, 1)
+    V.tensor_scalar(T.rep192[0:K, :], T.er[0:K, :], 64.0, T.d192[0:K, 0:1], A.is_equal, A.mult).then_inc(s_r192, 1)
+    V.tensor_scalar(T.rep[0:K, :], T.er[0:K, :], 64.0, None, A.is_equal).then_inc(s_rep, 1)
+
+    s_dd, s_mm, s_ps1, s_sc, s_pr, s_ps2, s_off, s_sct = [new() for _ in range(8)]
+    V.wait_ge(T.sem.kld, 16 * N)
+    V.tensor_scalar(T.dd[0:K, :], T.kk[0:K, :], 10, None, A.arith_shift_right).then_inc(s_dd, 1)
+    V.wait_ge(s_dd, 1)
+    V.wait_ge(s_dcol, 1)
+    V.tensor_scalar(T.mm[0:K, 1:33], T.dd[0:K, :], T.dcol[0:K, 0:1], None, A.is_equal).then_inc(s_mm, 1)
+
+    PE.wait_ge(s_mm, 1)
+    PE.wait_ge(s_m0, 1)
+    PE.wait_ge(s_a1, 1)
+    PE.wait_ge(s_a2, 1)
+    PE.matmul(T.ps1[0:K, 0:32], T.a1[0:K, :], T.mm[0:K, 1:33], True, False)
+    PE.matmul(T.ps1[0:K, 0:32], T.a2[0:K, :], T.mm[0:K, 0:32], False, True).then_inc(s_ps1, 1)
+    PE.wait_ge(s_r192, 1)
+    PE.matmul(T.ps2[:, 0:32], T.rep192[0:K, :], T.mm[0:K, 1:33], True, False)
+
+    V.wait_ge(s_ps1, 1)
+    V.wait_ge(s_z0, 1)
+    V.tensor_tensor_scan(T.sc[0:K, :], T.z0[0:K, :], T.ps1[0:K, 0:32], 0.0, A.add, A.add).then_inc(s_sc, 1)
+    V.wait_ge(s_sc, 1)
+    V.wait_ge(s_mm, 1)
+    V.tensor_tensor(T.pr[0:K, :], T.sc[0:K, :], T.mm[0:K, 1:33], A.mult).then_inc(s_pr, 1)
+
+    PE.wait_ge(s_pr, 1)
+    PE.wait_ge(s_rep, 1)
+    PE.matmul(T.ps2[:, 0:32], T.rep[0:K, :], T.pr[0:K, :], False, True).then_inc(s_ps2, 1)
+
+    V.wait_ge(s_ps2, 1)
+    V.tensor_copy(T.off[:, :], T.ps2[:, 0:32]).then_inc(s_off, 1)
+    V.wait_ge(s_off, 1)
+    V.wait_ge(T.sem.xld, 16)
+    V.wait_ge(s_wv, 1)
+    V.wait_ge(s_wg, 1)
+    V.tensor_copy(T.win[:, 0:WIN].indirect(T.off[:, 0:32]), T.xs[:, :]).then_inc(s_sct, 1)
+
+    def hops(s):
+        a, b = topo.chip(core), topo.chip(T.cores[(rank + s) % N])
+        return 1 if (topo.same_plane(a, b) or topo.mates(a, b)) else 2
+    shifts = sorted(range(1, N), key=lambda s: (-hops(s), s))
+
+    def blk(t, i):
+        return t[:, CAP * i:CAP * (i + 1)]
+
+    g.wait_ge(s_sct, 1)
+    sent = 0
+    for s in shifts:
+        d = (rank + s) % N
+        dst = T.cores[d]
+        rid, pid, _se = topo.addr(dst)
+        mask = topo.mask(core, dst)
+        g.remote_dma(blk(T.land, rank), blk(T.win, d), T.sem["arr%d" % rank], T.sem.sent, pid, rid, mask)
+        sent += bin(mask).count("1")
+
+    SY.wait_ge(s_sct, 1)
+    SY.dma_start(blk(T.y, rank), blk(T.win, rank)).then_inc(T.sem.st, 16)
+    for t, s in enumerate(shifts):
+        src = (rank - s) % N
+        q = SC if t % 2 else SY
+        q.wait_ge(T.sem["arr%d" % src], bin(topo.mask(T.cores[src], core)).count("1"))
+        q.dma_start(blk(T.y, src), blk(T.land, src)).then_inc(T.sem.st, 16)
+
+    g.wait_ge(T.sem.sent, sent)
+    g.wait_ge(T.sem.st, 16 * N)

@@ -1,4 +1,4 @@
-from concourse.mybir import AluOpType
+from concourse.mybir import AluOpType, ActivationFunctionType
 
 N = 4
 CAP = 192
@@ -7,8 +7,11 @@ WIN = N * CAP
 
 SCRATCH = {
     "xs": ("sbuf", [128, COLS], "bfloat16"),
+    "xp": ("sbuf", [128, COLS], "bfloat16"),
     "win": ("sbuf", [128, WIN], "bfloat16"),
+    "win2": ("sbuf", [128, WIN], "bfloat16"),
     "land": ("sbuf", [128, WIN], "bfloat16"),
+    "zz": ("sbuf", [128, CAP], "bfloat16"),
     "kk": ("sbuf", [128, 32], "int32"),
     "dd": ("sbuf", [128, 32], "int32"),
     "mm": ("sbuf", [128, 33], "bfloat16"),
@@ -27,10 +30,11 @@ SCRATCH = {
     "sc": ("sbuf", [128, 32], "float32"),
     "pr": ("sbuf", [128, 32], "bfloat16"),
     "off": ("sbuf", [128, 32], "uint16"),
+    "offp": ("sbuf", [128, 32], "uint16"),
     "ps1": ("psum", [128, 512], "float32"),
     "ps2": ("psum", [128, 512], "float32"),
 }
-SEMAPHORES = ["s%d" % i for i in range(32)] + ["kld", "xld", "st", "sent"] + ["arr%d" % i for i in range(N)]
+SEMAPHORES = ["s%d" % i for i in range(36)] + ["kld", "xld", "st", "sent", "arrp"] + ["arr%d" % i for i in range(N)]
 
 
 def rank_program(g, core, T, topo):
@@ -45,6 +49,17 @@ def rank_program(g, core, T, topo):
         used[0] += 1
         return T.sem["s%d" % (used[0] - 1)]
 
+    def blk(t, i):
+        return t[:, CAP * i:CAP * (i + 1)]
+
+    def plane_peer(r):
+        c = topo.chip(T.cores[r])
+        return [d for d in range(N) if d != r and topo.same_plane(c, topo.chip(T.cores[d]))][0]
+
+    def engines(src, dst):
+        return bin(topo.mask(src, dst)).count("1")
+
+    peer = plane_peer(rank)
     K = 4 * 16
 
     for d in range(N):
@@ -52,16 +67,20 @@ def rank_program(g, core, T, topo):
         q.dma_start(T.kk[d:K:4, :], T.key[:, :]).then_inc(T.sem.kld, 16)
     SY.dma_start(T.xs[:, :], T.x[:, :]).then_inc(T.sem.xld, 16)
 
-    s_ta, s_tr, s_wg = new(), new(), new()
+    s_ta, s_tr = new(), new()
     g.iota(T.ta[0:K, :], [[-1, 64]], 64, 1).then_inc(s_ta, 1)
     g.iota(T.tr[0:K, :], [[0, 8], [4, 16]], 67, -1).then_inc(s_tr, 1)
-    half = WIN // 2
-    g.iota(T.win[:, half:WIN], [[0, WIN - half]], 0, 0, allow_small_or_imprecise_dtypes=True).then_inc(s_wg, 1)
 
-    s_m0, s_z0, s_wv = new(), new(), new()
+    s_zz, s_m0, s_z0, s_zw, s_z2 = new(), new(), new(), new(), new()
+    V.memset(T.zz[:, :], 0.0).then_inc(s_zz, 1)
     V.memset(T.mm[0:K, 0:1], 0.0).then_inc(s_m0, 1)
     V.memset(T.z0[0:K, :], 0.0).then_inc(s_z0, 1)
-    V.memset(T.win[:, 0:half], 0.0).then_inc(s_wv, 1)
+    SC.wait_ge(s_zz, 1)
+    for i in range(N):
+        SC.activation(blk(T.win, i), T.zz[:, :], ActivationFunctionType.Copy).then_inc(s_zw, 1)
+    for i in range(N):
+        SC.activation(blk(T.win2, i), T.zz[:, :], ActivationFunctionType.Copy).then_inc(s_z2, 1)
+
     s_di, s_ea, s_dcol, s_d192, s_a1, s_a2, s_er, s_r192, s_rep = [new() for _ in range(9)]
     V.wait_ge(s_ta, 1)
     V.tensor_scalar(T.di[0:K, :], T.ta[0:K, 0:1], 3, None, A.bitwise_and).then_inc(s_di, 1)
@@ -79,7 +98,7 @@ def rank_program(g, core, T, topo):
     V.tensor_scalar(T.rep192[0:K, :], T.er[0:K, :], 64.0, T.d192[0:K, 0:1], A.is_equal, A.mult).then_inc(s_r192, 1)
     V.tensor_scalar(T.rep[0:K, :], T.er[0:K, :], 64.0, None, A.is_equal).then_inc(s_rep, 1)
 
-    s_dd, s_mm, s_ps1, s_sc, s_pr, s_ps2, s_off, s_sct = [new() for _ in range(8)]
+    s_dd, s_mm, s_ps1, s_sc, s_pr, s_ps2, s_off, s_sct, s_sct2 = [new() for _ in range(9)]
     V.wait_ge(T.sem.kld, 16 * N)
     V.tensor_scalar(T.dd[0:K, :], T.kk[0:K, :], 10, None, A.arith_shift_right).then_inc(s_dd, 1)
     V.wait_ge(s_dd, 1)
@@ -110,35 +129,41 @@ def rank_program(g, core, T, topo):
     V.tensor_copy(T.off[:, :], T.ps2[:, 0:32]).then_inc(s_off, 1)
     V.wait_ge(s_off, 1)
     V.wait_ge(T.sem.xld, 16)
-    V.wait_ge(s_wv, 1)
-    V.wait_ge(s_wg, 1)
+    V.wait_ge(s_zw, N)
     V.tensor_copy(T.win[:, 0:WIN].indirect(T.off[:, 0:32]), T.xs[:, :]).then_inc(s_sct, 1)
+    V.wait_ge(T.sem.arrp, 2 * engines(T.cores[peer], core))
+    V.wait_ge(s_z2, N)
+    V.tensor_copy(T.win2[:, 0:WIN].indirect(T.offp[:, 0:32]), T.xp[:, :]).then_inc(s_sct2, 1)
 
-    def hops(s):
-        a, b = topo.chip(core), topo.chip(T.cores[(rank + s) % N])
-        return 1 if (topo.same_plane(a, b) or topo.mates(a, b)) else 2
-    shifts = sorted(range(1, N), key=lambda s: (-hops(s), s))
-
-    def blk(t, i):
-        return t[:, CAP * i:CAP * (i + 1)]
-
-    g.wait_ge(s_sct, 1)
     sent = 0
+    p_rid, p_pid, _se = topo.addr(T.cores[peer])
+    p_mask = topo.mask(core, T.cores[peer])
+    g.wait_ge(T.sem.xld, 16)
+    g.remote_dma(T.xp[:, :], T.xs[:, :], T.sem.arrp, T.sem.sent, p_pid, p_rid, p_mask)
+    sent += engines(core, T.cores[peer])
+    g.wait_ge(s_off, 1)
+    g.remote_dma(T.offp[:, :], T.off[:, :], T.sem.arrp, T.sem.sent, p_pid, p_rid, p_mask)
+    sent += engines(core, T.cores[peer])
+    shifts = [s for s in range(1, N) if (rank + s) % N != peer]
+    g.wait_ge(s_sct, 1)
     for s in shifts:
         d = (rank + s) % N
         dst = T.cores[d]
         rid, pid, _se = topo.addr(dst)
-        mask = topo.mask(core, dst)
-        g.remote_dma(blk(T.land, rank), blk(T.win, d), T.sem["arr%d" % rank], T.sem.sent, pid, rid, mask)
-        sent += bin(mask).count("1")
+        g.remote_dma(blk(T.land, rank), blk(T.win, d), T.sem["arr%d" % rank], T.sem.sent, pid, rid,
+                     topo.mask(core, dst))
+        sent += engines(core, dst)
 
-    SY.wait_ge(s_sct, 1)
+    srcs = [(rank - s) % N for s in range(1, N) if plane_peer((rank - s) % N) != rank]
+    first, second = srcs
+    SY.wait_ge(T.sem["arr%d" % first], engines(T.cores[first], core))
+    SY.dma_start(blk(T.y, first), blk(T.land, first)).then_inc(T.sem.st, 16)
+    SY.wait_ge(T.sem.sent, sent)
     SY.dma_start(blk(T.y, rank), blk(T.win, rank)).then_inc(T.sem.st, 16)
-    for t, s in enumerate(shifts):
-        src = (rank - s) % N
-        q = SC if t % 2 else SY
-        q.wait_ge(T.sem["arr%d" % src], bin(topo.mask(T.cores[src], core)).count("1"))
-        q.dma_start(blk(T.y, src), blk(T.land, src)).then_inc(T.sem.st, 16)
+    SY.wait_ge(s_sct2, 1)
+    SY.dma_start(blk(T.y, peer), blk(T.win2, rank)).then_inc(T.sem.st, 16)
+    SC.wait_ge(T.sem["arr%d" % second], engines(T.cores[second], core))
+    SC.dma_start(blk(T.y, second), blk(T.land, second)).then_inc(T.sem.st, 16)
 
     g.wait_ge(T.sem.sent, sent)
     g.wait_ge(T.sem.st, 16 * N)

from concourse.mybir import AluOpType, ActivationFunctionType

N = 4
CAP = 192
COLS = 512
WIN = N * CAP

SCRATCH = {
    "xs": ("sbuf", [128, COLS], "bfloat16"),
    "xp": ("sbuf", [128, COLS], "bfloat16"),
    "win": ("sbuf", [128, WIN], "bfloat16"),
    "win2": ("sbuf", [128, WIN], "bfloat16"),
    "land": ("sbuf", [128, WIN], "bfloat16"),
    "zz": ("sbuf", [128, CAP], "bfloat16"),
    "kk": ("sbuf", [128, 32], "int32"),
    "dd": ("sbuf", [128, 32], "int32"),
    "mm": ("sbuf", [128, 33], "bfloat16"),
    "z0": ("sbuf", [128, 32], "float32"),
    "ta": ("sbuf", [128, 64], "int32"),
    "ea": ("sbuf", [128, 64], "int32"),
    "a1": ("sbuf", [128, 64], "bfloat16"),
    "a2": ("sbuf", [128, 64], "bfloat16"),
    "tr": ("sbuf", [128, 128], "int32"),
    "er": ("sbuf", [128, 128], "int32"),
    "rep": ("sbuf", [128, 128], "bfloat16"),
    "rep192": ("sbuf", [128, 128], "bfloat16"),
    "di": ("sbuf", [128, 1], "int32"),
    "dcol": ("sbuf", [128, 1], "float32"),
    "d192": ("sbuf", [128, 1], "float32"),
    "sc": ("sbuf", [128, 32], "float32"),
    "pr": ("sbuf", [128, 32], "bfloat16"),
    "off": ("sbuf", [128, 32], "uint16"),
    "offp": ("sbuf", [128, 32], "uint16"),
    "ps1": ("psum", [128, 512], "float32"),
    "ps2": ("psum", [128, 512], "float32"),
}
SEMAPHORES = ["s%d" % i for i in range(36)] + ["kld", "xld", "st", "sent", "arrp"] + ["arr%d" % i for i in range(N)]


def rank_program(g, core, T, topo):
    rank = T.rank_of(core)
    if rank is None:
        return
    V, PE, SY, SC = g.vector, g.tensor, g.sync, g.scalar
    A = AluOpType
    used = [0]

    def new():
        used[0] += 1
        return T.sem["s%d" % (used[0] - 1)]

    def blk(t, i):
        return t[:, CAP * i:CAP * (i + 1)]

    def plane_peer(r):
        c = topo.chip(T.cores[r])
        return [d for d in range(N) if d != r and topo.same_plane(c, topo.chip(T.cores[d]))][0]

    def engines(src, dst):
        return bin(topo.mask(src, dst)).count("1")

    peer = plane_peer(rank)
    K = 4 * 16

    for d in range(N):
        q = SY if d < 2 else SC
        q.dma_start(T.kk[d:K:4, :], T.key[:, :]).then_inc(T.sem.kld, 16)
    SY.dma_start(T.xs[:, :], T.x[:, :]).then_inc(T.sem.xld, 16)

    s_ta, s_tr = new(), new()
    g.iota(T.ta[0:K, :], [[-1, 64]], 64, 1).then_inc(s_ta, 1)
    g.iota(T.tr[0:K, :], [[0, 8], [4, 16]], 67, -1).then_inc(s_tr, 1)

    s_zz, s_m0, s_z0, s_zw, s_z2 = new(), new(), new(), new(), new()
    V.memset(T.zz[:, :], 0.0).then_inc(s_zz, 1)
    V.memset(T.mm[0:K, 0:1], 0.0).then_inc(s_m0, 1)
    V.memset(T.z0[0:K, :], 0.0).then_inc(s_z0, 1)
    SC.wait_ge(s_zz, 1)
    for i in range(N):
        SC.activation(blk(T.win, i), T.zz[:, :], ActivationFunctionType.Copy).then_inc(s_zw, 1)
    for i in range(N):
        SC.activation(blk(T.win2, i), T.zz[:, :], ActivationFunctionType.Copy).then_inc(s_z2, 1)

    s_di, s_ea, s_dcol, s_d192, s_a1, s_a2, s_er, s_r192, s_rep = [new() for _ in range(9)]
    V.wait_ge(s_ta, 1)
    V.tensor_scalar(T.di[0:K, :], T.ta[0:K, 0:1], 3, None, A.bitwise_and).then_inc(s_di, 1)
    V.tensor_scalar(T.ea[0:K, :], T.ta[0:K, :], 67, None, A.bitwise_and).then_inc(s_ea, 1)
    V.wait_ge(s_di, 1)
    V.tensor_copy(T.dcol[0:K, :], T.di[0:K, :]).then_inc(s_dcol, 1)
    V.tensor_scalar(T.d192[0:K, :], T.di[0:K, :], float(CAP), None, A.mult).then_inc(s_d192, 1)
    V.wait_ge(s_ea, 1)
    V.tensor_scalar(T.a1[0:K, :], T.ea[0:K, :], 0.0, None, A.is_equal).then_inc(s_a1, 1)
    V.tensor_scalar(T.a2[0:K, :], T.ea[0:K, :], 64.0, None, A.is_equal).then_inc(s_a2, 1)
    V.wait_ge(s_tr, 1)
    V.tensor_scalar(T.er[0:K, :], T.tr[0:K, :], 124, None, A.bitwise_and).then_inc(s_er, 1)
    V.wait_ge(s_er, 1)
    V.wait_ge(s_d192, 1)
    V.tensor_scalar(T.rep192[0:K, :], T.er[0:K, :], 64.0, T.d192[0:K, 0:1], A.is_equal, A.mult).then_inc(s_r192, 1)
    V.tensor_scalar(T.rep[0:K, :], T.er[0:K, :], 64.0, None, A.is_equal).then_inc(s_rep, 1)

    s_dd, s_mm, s_ps1, s_sc, s_pr, s_ps2, s_off, s_sct, s_sct2 = [new() for _ in range(9)]
    V.wait_ge(T.sem.kld, 16 * N)
    V.tensor_scalar(T.dd[0:K, :], T.kk[0:K, :], 10, None, A.arith_shift_right).then_inc(s_dd, 1)
    V.wait_ge(s_dd, 1)
    V.wait_ge(s_dcol, 1)
    V.tensor_scalar(T.mm[0:K, 1:33], T.dd[0:K, :], T.dcol[0:K, 0:1], None, A.is_equal).then_inc(s_mm, 1)

    PE.wait_ge(s_mm, 1)
    PE.wait_ge(s_m0, 1)
    PE.wait_ge(s_a1, 1)
    PE.wait_ge(s_a2, 1)
    PE.matmul(T.ps1[0:K, 0:32], T.a1[0:K, :], T.mm[0:K, 1:33], True, False)
    PE.matmul(T.ps1[0:K, 0:32], T.a2[0:K, :], T.mm[0:K, 0:32], False, True).then_inc(s_ps1, 1)
    PE.wait_ge(s_r192, 1)
    PE.matmul(T.ps2[:, 0:32], T.rep192[0:K, :], T.mm[0:K, 1:33], True, False)

    V.wait_ge(s_ps1, 1)
    V.wait_ge(s_z0, 1)
    V.tensor_tensor_scan(T.sc[0:K, :], T.z0[0:K, :], T.ps1[0:K, 0:32], 0.0, A.add, A.add).then_inc(s_sc, 1)
    V.wait_ge(s_sc, 1)
    V.wait_ge(s_mm, 1)
    V.tensor_tensor(T.pr[0:K, :], T.sc[0:K, :], T.mm[0:K, 1:33], A.mult).then_inc(s_pr, 1)

    PE.wait_ge(s_pr, 1)
    PE.wait_ge(s_rep, 1)
    PE.matmul(T.ps2[:, 0:32], T.rep[0:K, :], T.pr[0:K, :], False, True).then_inc(s_ps2, 1)

    V.wait_ge(s_ps2, 1)
    V.tensor_copy(T.off[:, :], T.ps2[:, 0:32]).then_inc(s_off, 1)
    V.wait_ge(s_off, 1)
    V.wait_ge(T.sem.xld, 16)
    V.wait_ge(s_zw, N)
    V.tensor_copy(T.win[:, 0:WIN].indirect(T.off[:, 0:32]), T.xs[:, :]).then_inc(s_sct, 1)
    V.wait_ge(T.sem.arrp, 2 * engines(T.cores[peer], core))
    V.wait_ge(s_z2, N)
    V.tensor_copy(T.win2[:, 0:WIN].indirect(T.offp[:, 0:32]), T.xp[:, :]).then_inc(s_sct2, 1)

    sent = 0
    p_rid, p_pid, _se = topo.addr(T.cores[peer])
    p_mask = topo.mask(core, T.cores[peer])
    g.wait_ge(T.sem.xld, 16)
    g.remote_dma(T.xp[:, :], T.xs[:, :], T.sem.arrp, T.sem.sent, p_pid, p_rid, p_mask)
    sent += engines(core, T.cores[peer])
    g.wait_ge(s_off, 1)
    g.remote_dma(T.offp[:, :], T.off[:, :], T.sem.arrp, T.sem.sent, p_pid, p_rid, p_mask)
    sent += engines(core, T.cores[peer])
    shifts = [s for s in range(1, N) if (rank + s) % N != peer]
    g.wait_ge(s_sct, 1)
    for s in shifts:
        d = (rank + s) % N
        dst = T.cores[d]
        rid, pid, _se = topo.addr(dst)
        g.remote_dma(blk(T.land, rank), blk(T.win, d), T.sem["arr%d" % rank], T.sem.sent, pid, rid,
                     topo.mask(core, dst))
        sent += engines(core, dst)

    srcs = [(rank - s) % N for s in range(1, N) if plane_peer((rank - s) % N) != rank]
    first, second = srcs
    SY.wait_ge(T.sem["arr%d" % first], engines(T.cores[first], core))
    SY.dma_start(blk(T.y, first), blk(T.land, first)).then_inc(T.sem.st, 16)
    SY.wait_ge(T.sem.sent, sent)
    SY.dma_start(blk(T.y, rank), blk(T.win, rank)).then_inc(T.sem.st, 16)
    SY.wait_ge(s_sct2, 1)
    SY.dma_start(blk(T.y, peer), blk(T.win2, rank)).then_inc(T.sem.st, 16)
    SC.wait_ge(T.sem["arr%d" % second], engines(T.cores[second], core))
    SC.dma_start(blk(T.y, second), blk(T.land, second)).then_inc(T.sem.st, 16)

    g.wait_ge(T.sem.sent, sent)
    g.wait_ge(T.sem.st, 16 * N)
